import numpy as np
import ml_dtypes


def mxq(x, axis, fmt="e4m3"):
    dtype, down = {"e4m3": (ml_dtypes.float8_e4m3fn, 7), "e5m2": (ml_dtypes.float8_e5m2, 14)}[fmt]
    v = np.moveaxis(np.asarray(x, np.float32).astype(ml_dtypes.bfloat16).astype(np.float64), axis, -1)
    blocks = v.reshape(v.shape[:-1] + (-1, 32))
    amax = np.abs(blocks).max(-1, keepdims=True)
    byte = np.maximum(np.where(amax > 0, np.frexp(amax)[1] - 1 + 127, 0) - down, 1)
    scale = np.exp2(byte - 127.0)
    codes = (blocks / scale).astype(np.float32).astype(dtype).astype(np.float64)
    return np.moveaxis((codes * scale).reshape(v.shape), -1, axis)


WIDE = False


def mx_kscale(k):
    if not WIDE:
        return np.ones(k)
    levels = np.array([10, -10, 5, -5, 0])
    if k % 512:
        return np.exp2(np.random.permutation(np.resize(levels, k // 32))).repeat(32)
    a = np.empty((k // 512, 16))
    for p in range(k // 512):
        a[p, :8] = np.random.permutation(np.resize(levels, 8))
        for g in range(8):
            far = levels[np.abs(levels - a[p, g]) >= 10]
            a[p, g + 8] = far[np.random.randint(len(far))]
    return np.exp2(a.ravel()).repeat(32)


def f64(x):
    return np.asarray(x).astype(np.float64)


def striped(idx):
    return np.tile(idx.reshape(-1, 16).T, (8, 1)).astype(np.uint16)


def unstriped(offs):
    return offs[:16].T.reshape(-1).astype(np.int64)


E2M1 = np.array([0.0, 0.5, 1.0, 1.5, 2.0, 3.0, 4.0, 6.0, -0.0, -0.5, -1.0, -1.5, -2.0, -3.0, -4.0, -6.0])


def pack_weight(w, fmt):
    k, n = w.shape
    w = f64(np.asarray(w, np.float32).astype(ml_dtypes.bfloat16)).reshape(k // 32, 32, n)
    amax = np.abs(w).max(1)
    if fmt == "e4m3":
        byte = np.frexp(amax)[1] - 1 + 127 - 7
    else:
        mant, ex = np.frexp(amax / 6.0)
        byte = np.where(mant > 0.5, ex, ex - 1) + 127
    byte = np.clip(np.where(amax > 0, byte, 1), 1, 254)
    scaled = (w * np.exp2(127.0 - byte)[:, None, :]).reshape(k, n).astype(np.float32)
    by_word = np.ascontiguousarray(scaled.reshape(k // 512, 128, 4, n).transpose(0, 1, 3, 2))
    if fmt == "e4m3":
        words = by_word.astype(ml_dtypes.float8_e4m3fn).view(np.uint8)
    else:
        c = by_word.astype(ml_dtypes.float4_e2m1fn).view(np.uint8) & 0xF
        words = (c[..., 0::2] | (c[..., 1::2] << 4)).reshape(k // 512, 128, 2 * n)
    return np.ascontiguousarray(words), np.ascontiguousarray(byte.astype(np.uint8).reshape(k // 512, 16, n))


def unpack_weight(words, scales, fmt):
    g, _, n = scales.shape
    words = np.ascontiguousarray(words).reshape(g, 128, n, -1)
    if fmt == "e4m3":
        vals = words.view(ml_dtypes.float8_e4m3fn).astype(np.float64)
    else:
        nib = np.empty((g, 128, n, 4), np.uint8)
        nib[..., 0::2] = words & 0xF
        nib[..., 1::2] = words >> 4
        vals = E2M1[nib]
    vals = vals * np.repeat(np.exp2(scales.astype(np.float64) - 127.0), 8, axis=1)[..., None]
    return vals.transpose(0, 1, 3, 2).reshape(g * 512, n)


def gelu(v):
    return 0.5 * v * (1.0 + np.tanh(np.sqrt(2.0 / np.pi) * (v + 0.044715 * v**3)))


K, K1, H, T, S, T3, S2 = 2048, 1024, 1024, 2048, 512, 1024, 512

def setup_inputs():
    n = np.random.standard_normal
    s = mx_kscale(K)[:, None]
    u = mx_kscale(H)[:, None]
    tab_words, tab_scales = pack_weight(n((K, T)) * s, "e4m3")
    tab2_words, tab2_scales = pack_weight(n((H, T3)) / u / np.sqrt(H), "e4m3")
    tab3_words, tab3_scales = pack_weight(n((H, T3)) / u / np.sqrt(H), "e4m3")
    w4_words, w4_scales = pack_weight(n((K - K1, H)) / s[K1:] / np.sqrt(K), "e2m1")
    return {
        "tab_words": tab_words, "tab_scales": tab_scales,
        "offs": striped(np.random.permutation(T)[:S]),
        "tab2_words": tab2_words, "tab2_scales": tab2_scales,
        "offs2": striped(np.random.permutation(T3)[:S2]),
        "tab3_words": tab3_words, "tab3_scales": tab3_scales,
        "offs3": striped(np.random.permutation(T3)[:S2]),
        "w1": (n((K1, H)) / s[:K1] / np.sqrt(K)).astype(np.float32),
        "w4_words": w4_words, "w4_scales": w4_scales,
        "level": n((H, S)).astype(np.float32),
        "gain": (np.exp(0.3 * n(H)) * u[:, 0]).astype(np.float32),
        "seat": n((S2, S)).astype(np.float32),
    }

def reference(tab_words, tab_scales, offs, tab2_words, tab2_scales, offs2, tab3_words, tab3_scales, offs3,
              w1, w4_words, w4_scales, level, gain, seat):
    v = unpack_weight(tab_words, tab_scales, "e4m3")[:, unstriped(offs)]
    v2 = unpack_weight(tab2_words, tab2_scales, "e4m3")[:, unstriped(offs2)]
    v3 = unpack_weight(tab3_words, tab3_scales, "e4m3")[:, unstriped(offs3)]
    w1q = mxq(f64(w1), 0, "e4m3")
    w4 = unpack_weight(w4_words, w4_scales, "e2m1")
    f = w1q.T @ v[:K1] + w4.T @ v[K1:]
    h = np.maximum(f, f64(level)) * f64(gain)[:, None]
    hq = mxq(h, 0, "e4m3")
    e2 = v2.T @ hq
    e3 = v3.T @ hq
    d = f64(seat)
    return np.maximum(e2 + d, e3 - d)

@@ -1,0 +1,250 @@
+from contextlib import ExitStack
+
+import concourse.mybir as mybir
+
+K, K1, H, T, S, T3, S2 = 2048, 1024, 1024, 2048, 512, 1024, 512
+FLOPS = 2 * K * H * S + 2 * 2 * H * S2 * S
+
+F32 = mybir.dt.float32
+BF16 = mybir.dt.bfloat16
+I32 = mybir.dt.int32
+U32 = mybir.dt.uint32
+U16 = mybir.dt.uint16
+U8 = mybir.dt.uint8
+FP8X4 = mybir.dt.float8_e4m3fn_x4
+FP4X4 = mybir.dt.float4_e2m1fn_x4
+ALU = mybir.AluOpType
+COPY = mybir.ActivationFunctionType.Copy
+
+P = 128
+PACK = 4
+KP = P * PACK
+QUADS = 4
+HALF = S // 2
+
+
+def tile_list_cockpit_pairing_comfort_kernel(
+    tc, tab_words, tab_scales, offs, tab2_words, tab2_scales, offs2, tab3_words, tab3_scales, offs3,
+    w1, w4_words, w4_scales, level, gain, seat, out,
+):
+    nc = tc.nc
+    with ExitStack() as ctx:
+        keep = ctx.enter_context(tc.tile_pool(name="keep", bufs=1))
+        ring = ctx.enter_context(tc.tile_pool(name="ring", bufs=2))
+        psum = ctx.enter_context(tc.psum_pool(name="psum", bufs=1))
+
+        def tile(name, shape, dtype, over=None):
+            return keep.tile(shape, dtype, name=name, tag=over or name, align_bytes=64)
+
+        def load(dst, src):
+            nc.sync.dma_start(out=dst, in_=src)
+
+        def load_raw(dst, src):
+            nc.sync.dma_start(out=dst.bitcast(I32), in_=src.bitcast(I32))
+
+        lists = [tile("list%d" % n, [P, S // 16], U16) for n in range(3)]
+        w4_sc_in = tile("w4_sc_in", [P, 2, H], U8)
+        tab_sc = tile("tab_sc", [P, 2, T], U8)
+        crew_sc = [tile("crew_sc%d" % n, [P, T3], U8) for n in range(2)]
+        nc.gpsimd.memset(w4_sc_in[:].bitcast(I32), 0)
+        nc.vector.memset(tab_sc[:].bitcast(I32), 0)
+        for n in range(2):
+            nc.gpsimd.memset(crew_sc[n][:].bitcast(I32), 0)
+
+        def quad_rows(q):
+            return slice(4 * q, 4 * q + 4)
+
+        small = []
+        for q in range(QUADS):
+            small.append((w4_sc_in[32 * q : 32 * q + 4, :, :], w4_scales[:, quad_rows(q), :].rearrange("a r c -> r a c")))
+        for q in range(QUADS):
+            small.append((tab_sc[32 * q : 32 * q + 4, :, :], tab_scales[2:4, quad_rows(q), :].rearrange("a r c -> r a c")))
+            small.append((tab_sc[32 * q + 4 : 32 * q + 8, :, :], tab_scales[0:2, quad_rows(q), :].rearrange("a r c -> r a c")))
+        for n, scales in enumerate((tab2_scales, tab3_scales)):
+            for q in range(QUADS):
+                small.append((crew_sc[n][32 * q : 32 * q + 8, :], scales[:, quad_rows(q), :]))
+
+        def load_small(first, last):
+            for dst, src in small[first:last]:
+                load_raw(dst, src)
+
+        w4_in = tile("w4_in", [P, 2, 2 * H], U8)
+        w1_in = [tile("w1_in%d" % g, [P, PACK, H], F32) for g in range(2)]
+        tab_w = [tile("tab_w%d" % g, [P, T], U32) for g in range(4)]
+        gains = tile("gains", [P, 2, PACK], F32)
+        lev = [[tile("lev%d%d" % (a, u), [P, 2, S], F32) for u in range(2)] for a in range(2)]
+        crew_w = [[tile("crew_w%d%d" % (n, a), [P, T3], U32) for a in range(2)] for n in range(2)]
+        seats = [tile("seats%d" % u, [P, 2, S], F32) for u in range(2)]
+
+        def load_w1(g, u):
+            rows = w1[KP * g : KP * (g + 1), :].rearrange("(p i) c -> p i c", i=PACK)
+            load(w1_in[g][:, 2 * u : 2 * u + 2, :], rows[:, 2 * u : 2 * u + 2, :])
+
+        def load_words(dst, words):
+            load_raw(dst[:], words.rearrange("p t i -> p (t i)"))
+
+        load(lists[0][:], offs)
+        load_raw(w4_in[:], w4_words.rearrange("a p n -> p a n"))
+        load(lists[1][:], offs2)
+        load(lists[2][:], offs3)
+        load(gains[:], gain.rearrange("(a p t) -> p a t", a=2, t=PACK))
+        load_w1(0, 0)
+        load_small(0, 6)
+        load_w1(0, 1)
+        load_small(6, 12)
+        load_w1(1, 0)
+        load_small(12, 18)
+        load_words(tab_w[2], tab_words[2])
+        load_small(18, 20)
+        load_w1(1, 1)
+        load_words(tab_w[3], tab_words[3])
+        load_words(tab_w[0], tab_words[0])
+        load_words(tab_w[1], tab_words[1])
+        for a in range(2):
+            rows = level[KP * a : KP * (a + 1), :].rearrange("(p t) j -> p t j", t=PACK)
+            for u in range(2):
+                load(lev[a][u][:], rows[:, 2 * u : 2 * u + 2, :])
+        for n, words in enumerate((tab2_words, tab3_words)):
+            for a in range(2):
+                load_words(crew_w[n][a], words[a])
+        for u in range(2):
+            load(seats[u][:], seat[2 * P * u : 2 * P * (u + 1), :].rearrange("(q p) j -> p q j", q=2))
+
+        w4_codes = tile("w4_codes", [P, 2, 2 * H], U8)
+        nc.vector.tensor_copy(
+            out=w4_codes[:].bitcast(U16).rearrange("p g (a t m) -> p (g a) m t", a=2, t=PACK),
+            in_=w4_in[:].bitcast(U16).rearrange("p g (a m t) -> p (g a) m t", a=2, t=PACK),
+        )
+
+        def gather(name, window, n, dtype, over):
+            picked = tile(name, [P, S], dtype, over)
+            nc.vector.tensor_copy(out=picked[:], in_=window.indirect(lists[n][:]))
+            return picked
+
+        w1_codes = [[None, None], [None, None]]
+        w1_sc = [[None, None], [None, None]]
+
+        def quantise_w1(g, a, over=None):
+            grouped = tile("w1_bf%d%d" % (g, a), [P, KP * PACK], BF16)
+            nc.scalar.copy(
+                out=grouped[:].rearrange("p (t m i) -> p m i t", t=PACK, i=PACK),
+                in_=w1_in[g][:, :, KP * a : KP * (a + 1)].rearrange("p i (m t) -> p m i t", t=PACK),
+            )
+            w1_codes[g][a] = tile("w1_codes%d%d" % (g, a), [P, KP], U32, over)
+            w1_sc[g][a] = tile("w1_sc%d%d" % (g, a), [P, KP], U8)
+            nc.vector.quantize_mx(out=w1_codes[g][a][:].bitcast(FP8X4), scales=w1_sc[g][a][:], in_=grouped[:])
+
+        v = [None] * 4
+        w4_sc = tile("w4_sc", [P, 2, H], U8)
+        nc.vector.tensor_copy(
+            out=w4_sc[:].rearrange("p g (a t m) -> p (g a) m t", a=2, t=PACK),
+            in_=w4_sc_in[:].rearrange("p g (a m t) -> p (g a) m t", a=2, t=PACK),
+        )
+        v_sc = [gather("v_sc0", tab_sc[:, 0, :], 0, U8, "w4_in"), gather("v_sc1", tab_sc[:, 1, :], 0, U8, "w4_sc_in")]
+        quantise_w1(0, 0, "tab_sc")
+        crew_scales = [gather("crew_scales0", crew_sc[0][:], 1, U8, "w1_bf00"), None]
+        v[2] = gather("v2", tab_w[2][:], 0, U32, "crew_sc0")
+        quantise_w1(0, 1, "tab_w2")
+        crew_scales[1] = gather("crew_scales1", crew_sc[1][:], 2, U8, "w1_bf01")
+        v[3] = gather("v3", tab_w[3][:], 0, U32, "crew_sc1")
+        quantise_w1(1, 0, "tab_w3")
+        v[0] = gather("v0", tab_w[0][:], 0, U32, "w1_bf10")
+        quantise_w1(1, 1, "tab_w0")
+        v[1] = gather("v1", tab_w[1][:], 0, U32, "w1_bf11")
+
+        f = [[psum.tile([P, S], F32, name="bank%d" % (PACK * a + t)) for t in range(PACK)] for a in range(2)]
+        for g in (2, 3, 0, 1):
+            for a in range(2):
+                for t in range(PACK):
+                    if g < 2:
+                        cols = slice(P * t, P * (t + 1))
+                        codes = w1_codes[g][a][:, cols].bitcast(FP8X4)
+                        scales = w1_sc[g][a][:, cols]
+                        rhs_scale = v_sc[g][4:P, :]
+                    else:
+                        c0 = KP * a + P * t
+                        codes = w4_codes[:, g - 2, 2 * c0 : 2 * (c0 + P)].bitcast(FP4X4)
+                        scales = w4_sc[:, g - 2, c0 : c0 + P]
+                        rhs_scale = v_sc[g - 2][:]
+                    nc.tensor.matmul_mx(
+                        out=f[a][t][:], lhsT=codes, lhsT_scale=scales,
+                        rhs=v[g][:].bitcast(FP8X4), rhs_scale=rhs_scale, start=(g == 2), stop=(g == 1),
+                    )
+
+        lifted = [[tile("lifted%d%d" % (a, t), [P, S], F32) for t in range(PACK)] for a in range(2)]
+        for a in range(2):
+            for t in range(PACK):
+                nc.vector.tensor_tensor(out=lifted[a][t][:], in0=f[a][t][:], in1=lev[a][t // 2][:, t % 2, :], op=ALU.max)
+
+        def make_h(a, j0, width, name):
+            scaled = tile("scaled" + name, [P, PACK, width], BF16)
+            for t in range(PACK):
+                nc.scalar.activation(
+                    out=scaled[:, t, :], in_=lifted[a][t][:, j0 : j0 + width], func=COPY, scale=gains[:, a, t : t + 1]
+                )
+            grouped = tile("h_bf" + name, [P, PACK * width], BF16)
+            nc.scalar.copy(
+                out=grouped[:].rearrange("p (c i t) -> p c t i", i=4, t=PACK),
+                in_=scaled[:].rearrange("p t (c i) -> p c t i", i=4),
+            )
+            return grouped
+
+        def quantise_h(grouped, width, name, over):
+            codes = tile("h_codes" + name, [P, width], U32, over)
+            scales = tile("h_sc" + name, [P, width], U8)
+            nc.vector.quantize_mx(out=codes[:].bitcast(FP8X4), scales=scales[:], in_=grouped[:])
+            return codes, scales
+
+        h_first = make_h(0, 0, S, "a")
+        h_second = [make_h(1, HALF * jh, HALF, "b%d" % jh) for jh in range(2)]
+        crew = [[None, None], [None, None]]
+        e = [
+            [[psum.tile([P, 2, HALF], F32, name="bank%d" % (4 * jh + 2 * n + u)) for u in range(2)] for n in range(2)]
+            for jh in range(2)
+        ]
+
+        def score(jh, n, a, codes, scales):
+            for u in range(2):
+                for q in range(2):
+                    cols = slice(P * (2 * u + q), P * (2 * u + q + 1))
+                    nc.tensor.matmul_mx(
+                        out=e[jh][n][u][:, q, :], lhsT=crew[n][a][:, cols].bitcast(FP8X4),
+                        lhsT_scale=crew_scales[n][4 * a : P, cols],
+                        rhs=codes.bitcast(FP8X4), rhs_scale=scales,
+                        start=(a, q) == (0, 0), stop=(a, q) == (1, 1),
+                    )
+
+        halves = [slice(HALF * jh, HALF * (jh + 1)) for jh in range(2)]
+        crew[0][0] = gather("crew00", crew_w[0][0][:], 1, U32, "lev10")
+        crew[0][1] = gather("crew01", crew_w[0][1][:], 1, U32, "lev11")
+        codes_a, scales_a = quantise_h(h_first, S, "a", None)
+        for jh in range(2):
+            score(jh, 0, 0, codes_a[:, halves[jh]], scales_a[:, halves[jh]])
+        crew[1][0] = gather("crew10", crew_w[1][0][:], 2, U32, "h_bfa")
+        for jh in range(2):
+            score(jh, 1, 0, codes_a[:, halves[jh]], scales_a[:, halves[jh]])
+        codes_b, scales_b = quantise_h(h_second[0], HALF, "b0", None)
+        score(0, 0, 1, codes_b[:], scales_b[:])
+        crew[1][1] = gather("crew11", crew_w[1][1][:], 2, U32, "h_bfb0")
+        score(0, 1, 1, codes_b[:], scales_b[:])
+
+        for jh in range(2):
+            jcols = halves[jh]
+            first = [ring.tile([P, 2, HALF], F32, name="first%d" % u) for u in range(2)]
+            for u in range(2):
+                nc.vector.scalar_tensor_tensor(
+                    out=first[u][:], in0=seats[u][:, :, jcols], scalar=2.0, in1=e[jh][0][u][:], op0=ALU.mult, op1=ALU.add
+                )
+            if jh == 0:
+                codes_b, scales_b = quantise_h(h_second[1], HALF, "b1", None)
+                for n in range(2):
+                    score(1, n, 1, codes_b[:], scales_b[:])
+            for u in range(2):
+                best = tile("best%d%d" % (jh, u), [P, 2, HALF], F32, "h_bfb1" if (jh, u) == (0, 1) else None)
+                nc.vector.tensor_tensor(out=best[:], in0=e[jh][1][u][:], in1=first[u][:], op=ALU.max)
+                result = ring.tile([P, 2, HALF], F32, name="result%d" % u)
+                engine = nc.vector if (jh, u) == (1, 1) else nc.gpsimd
+                engine.tensor_tensor(out=result[:], in0=best[:], in1=seats[u][:, :, jcols], op=ALU.subtract)
+                nc.sync.dma_start(
+                    out=out[2 * P * u : 2 * P * (u + 1), jcols].rearrange("(q p) j -> p q j", q=2), in_=result[:]
+                )

@@ -48,25 +48,25 @@ def tile_list_cockpit_pairing_comfort_kernel(
         crew_sc = [tile("crew_sc%d" % n, [P, T3], U8) for n in range(2)]
         nc.gpsimd.memset(w4_sc_in[:].bitcast(I32), 0)
         nc.vector.memset(tab_sc[:].bitcast(I32), 0)
-        for n in range(2):
-            nc.gpsimd.memset(crew_sc[n][:].bitcast(I32), 0)
-
-        def quad_rows(q):
-            return slice(4 * q, 4 * q + 4)
+        nc.gpsimd.memset(crew_sc[1][:].bitcast(I32), 0)
+        nc.vector.memset(crew_sc[0][:].bitcast(I32), 0)
 
         small = []
-        for q in range(QUADS):
-            small.append((w4_sc_in[32 * q : 32 * q + 4, :, :], w4_scales[:, quad_rows(q), :].rearrange("a r c -> r a c")))
-        for q in range(QUADS):
-            small.append((tab_sc[32 * q : 32 * q + 4, :, :], tab_scales[2:4, quad_rows(q), :].rearrange("a r c -> r a c")))
-            small.append((tab_sc[32 * q + 4 : 32 * q + 8, :, :], tab_scales[0:2, quad_rows(q), :].rearrange("a r c -> r a c")))
+        for r in range(4):
+            small.append((w4_sc_in[r:P:32, :, :], w4_scales[:, r:16:4, :].rearrange("a q c -> q a c")))
+        for r in range(4):
+            small.append((tab_sc[r:P:32, :, :], tab_scales[2:4, r:16:4, :].rearrange("a q c -> q a c")))
+            small.append((tab_sc[4 + r : P : 32, :, :], tab_scales[0:2, r:16:4, :].rearrange("a q c -> q a c")))
         for n, scales in enumerate((tab2_scales, tab3_scales)):
             for q in range(QUADS):
-                small.append((crew_sc[n][32 * q : 32 * q + 8, :], scales[:, quad_rows(q), :]))
+                small.append((crew_sc[n][32 * q + 8 : 32 * q + 16, :], scales[:, 4 * q : 4 * q + 4, :]))
 
         def load_small(first, last):
             for dst, src in small[first:last]:
                 load_raw(dst, src)
+
+        for dst, src in small[16:20]:
+            nc.gpsimd.dma_start(out=dst.bitcast(I32), in_=src.bitcast(I32))
 
         w4_in = tile("w4_in", [P, 2, 2 * H], U8)
         w1_in = [tile("w1_in%d" % g, [P, PACK, H], F32) for g in range(2)]
@@ -91,12 +91,11 @@ def tile_list_cockpit_pairing_comfort_kernel(
         load_w1(0, 0)
         load_small(0, 6)
         load_w1(0, 1)
-        load_small(6, 12)
         load_w1(1, 0)
-        load_small(12, 18)
+        load_small(6, 12)
         load_words(tab_w[2], tab_words[2])
-        load_small(18, 20)
         load_w1(1, 1)
+        load_small(12, 16)
         load_words(tab_w[3], tab_words[3])
         load_words(tab_w[0], tab_words[0])
         load_words(tab_w[1], tab_words[1])
@@ -112,8 +111,8 @@ def tile_list_cockpit_pairing_comfort_kernel(
 
         w4_codes = tile("w4_codes", [P, 2, 2 * H], U8)
         nc.vector.tensor_copy(
-            out=w4_codes[:].bitcast(U16).rearrange("p g (a t m) -> p (g a) m t", a=2, t=PACK),
-            in_=w4_in[:].bitcast(U16).rearrange("p g (a m t) -> p (g a) m t", a=2, t=PACK),
+            out=w4_codes[:].bitcast(U16).rearrange("p g (a t m) -> p (g a) t m", a=2, t=PACK),
+            in_=w4_in[:].bitcast(U16).rearrange("p g (a m t) -> p (g a) t m", a=2, t=PACK),
         )
 
         def gather(name, window, n, dtype, over):
@@ -127,8 +126,8 @@ def tile_list_cockpit_pairing_comfort_kernel(
         def quantise_w1(g, a, over=None):
             grouped = tile("w1_bf%d%d" % (g, a), [P, KP * PACK], BF16)
             nc.scalar.copy(
-                out=grouped[:].rearrange("p (t m i) -> p m i t", t=PACK, i=PACK),
-                in_=w1_in[g][:, :, KP * a : KP * (a + 1)].rearrange("p i (m t) -> p m i t", t=PACK),
+                out=grouped[:].rearrange("p (t m i) -> p m t i", t=PACK, i=PACK),
+                in_=w1_in[g][:, :, KP * a : KP * (a + 1)].rearrange("p i (m t) -> p m t i", t=PACK),
             )
             w1_codes[g][a] = tile("w1_codes%d%d" % (g, a), [P, KP], U32, over)
             w1_sc[g][a] = tile("w1_sc%d%d" % (g, a), [P, KP], U8)
@@ -137,16 +136,16 @@ def tile_list_cockpit_pairing_comfort_kernel(
         v = [None] * 4
         w4_sc = tile("w4_sc", [P, 2, H], U8)
         nc.vector.tensor_copy(
-            out=w4_sc[:].rearrange("p g (a t m) -> p (g a) m t", a=2, t=PACK),
-            in_=w4_sc_in[:].rearrange("p g (a m t) -> p (g a) m t", a=2, t=PACK),
+            out=w4_sc[:].rearrange("p g (a t m) -> p (g a) t m", a=2, t=PACK),
+            in_=w4_sc_in[:].rearrange("p g (a m t) -> p (g a) t m", a=2, t=PACK),
         )
-        v_sc = [gather("v_sc0", tab_sc[:, 0, :], 0, U8, "w4_in"), gather("v_sc1", tab_sc[:, 1, :], 0, U8, "w4_sc_in")]
-        quantise_w1(0, 0, "tab_sc")
-        crew_scales = [gather("crew_scales0", crew_sc[0][:], 1, U8, "w1_bf00"), None]
-        v[2] = gather("v2", tab_w[2][:], 0, U32, "crew_sc0")
+        quantise_w1(0, 0)
+        crew_scales = [None, gather("crew_scales1", crew_sc[1][:], 2, U8, "w4_sc_in")]
+        v_sc = [gather("v_sc0", tab_sc[:, 0, :], 0, U8, "crew_sc1"), gather("v_sc1", tab_sc[:, 1, :], 0, U8, "w4_in")]
+        v[2] = gather("v2", tab_w[2][:], 0, U32, "tab_sc")
         quantise_w1(0, 1, "tab_w2")
-        crew_scales[1] = gather("crew_scales1", crew_sc[1][:], 2, U8, "w1_bf01")
-        v[3] = gather("v3", tab_w[3][:], 0, U32, "crew_sc1")
+        crew_scales[0] = gather("crew_scales0", crew_sc[0][:], 1, U8, "w1_bf01")
+        v[3] = gather("v3", tab_w[3][:], 0, U32, "crew_sc0")
         quantise_w1(1, 0, "tab_w3")
         v[0] = gather("v0", tab_w[0][:], 0, U32, "w1_bf10")
         quantise_w1(1, 1, "tab_w0")
@@ -184,8 +183,8 @@ def tile_list_cockpit_pairing_comfort_kernel(
                 )
             grouped = tile("h_bf" + name, [P, PACK * width], BF16)
             nc.scalar.copy(
-                out=grouped[:].rearrange("p (c i t) -> p c t i", i=4, t=PACK),
-                in_=scaled[:].rearrange("p t (c i) -> p c t i", i=4),
+                out=grouped[:].rearrange("p (j t) -> p j t", t=PACK),
+                in_=scaled[:].rearrange("p t j -> p j t"),
             )
             return grouped
 
@@ -209,7 +208,7 @@ def tile_list_cockpit_pairing_comfort_kernel(
                     cols = slice(P * (2 * u + q), P * (2 * u + q + 1))
                     nc.tensor.matmul_mx(
                         out=e[jh][n][u][:, q, :], lhsT=crew[n][a][:, cols].bitcast(FP8X4),
-                        lhsT_scale=crew_scales[n][4 * a : P, cols],
+                        lhsT_scale=crew_scales[n][8 + 4 * a : P, cols],
                         rhs=codes.bitcast(FP8X4), rhs_scale=scales,
                         start=(a, q) == (0, 0), stop=(a, q) == (1, 1),
                     )

from contextlib import ExitStack

import concourse.mybir as mybir

K, K1, H, T, S, T3, S2 = 2048, 1024, 1024, 2048, 512, 1024, 512
FLOPS = 2 * K * H * S + 2 * 2 * H * S2 * S

F32 = mybir.dt.float32
BF16 = mybir.dt.bfloat16
I32 = mybir.dt.int32
U32 = mybir.dt.uint32
U16 = mybir.dt.uint16
U8 = mybir.dt.uint8
FP8X4 = mybir.dt.float8_e4m3fn_x4
FP4X4 = mybir.dt.float4_e2m1fn_x4
ALU = mybir.AluOpType
COPY = mybir.ActivationFunctionType.Copy

P = 128
PACK = 4
KP = P * PACK
QUADS = 4
HALF = S // 2


def tile_list_cockpit_pairing_comfort_kernel(
    tc, tab_words, tab_scales, offs, tab2_words, tab2_scales, offs2, tab3_words, tab3_scales, offs3,
    w1, w4_words, w4_scales, level, gain, seat, out,
):
    nc = tc.nc
    with ExitStack() as ctx:
        keep = ctx.enter_context(tc.tile_pool(name="keep", bufs=1))
        ring = ctx.enter_context(tc.tile_pool(name="ring", bufs=2))
        psum = ctx.enter_context(tc.psum_pool(name="psum", bufs=1))

        def tile(name, shape, dtype, over=None):
            return keep.tile(shape, dtype, name=name, tag=over or name, align_bytes=64)

        def load(dst, src):
            nc.sync.dma_start(out=dst, in_=src)

        def load_raw(dst, src):
            nc.sync.dma_start(out=dst.bitcast(I32), in_=src.bitcast(I32))

        lists = [tile("list%d" % n, [P, S // 16], U16) for n in range(3)]
        w4_sc_in = tile("w4_sc_in", [P, 2, H], U8)
        tab_sc = tile("tab_sc", [P, 2, T], U8)
        crew_sc = [tile("crew_sc%d" % n, [P, T3], U8) for n in range(2)]
        nc.gpsimd.memset(w4_sc_in[:].bitcast(I32), 0)
        nc.vector.memset(tab_sc[:].bitcast(I32), 0)
        nc.gpsimd.memset(crew_sc[1][:].bitcast(I32), 0)
        nc.vector.memset(crew_sc[0][:].bitcast(I32), 0)

        small = []
        for r in range(4):
            small.append((w4_sc_in[r:P:32, :, :], w4_scales[:, r:16:4, :].rearrange("a q c -> q a c")))
        for r in range(4):
            small.append((tab_sc[r:P:32, :, :], tab_scales[2:4, r:16:4, :].rearrange("a q c -> q a c")))
            small.append((tab_sc[4 + r : P : 32, :, :], tab_scales[0:2, r:16:4, :].rearrange("a q c -> q a c")))
        for n, scales in enumerate((tab2_scales, tab3_scales)):
            for q in range(QUADS):
                small.append((crew_sc[n][32 * q + 8 : 32 * q + 16, :], scales[:, 4 * q : 4 * q + 4, :]))

        def load_small(first, last):
            for dst, src in small[first:last]:
                load_raw(dst, src)

        for dst, src in small[16:20]:
            nc.gpsimd.dma_start(out=dst.bitcast(I32), in_=src.bitcast(I32))

        w4_in = tile("w4_in", [P, 2, 2 * H], U8)
        w1_in = [tile("w1_in%d" % g, [P, PACK, H], F32) for g in range(2)]
        tab_w = [tile("tab_w%d" % g, [P, T], U32) for g in range(4)]
        gains = tile("gains", [P, 2, PACK], F32)
        lev = [[tile("lev%d%d" % (a, u), [P, 2, S], F32) for u in range(2)] for a in range(2)]
        crew_w = [[tile("crew_w%d%d" % (n, a), [P, T3], U32) for a in range(2)] for n in range(2)]
        seats = [tile("seats%d" % u, [P, 2, S], F32) for u in range(2)]

        def load_w1(g, u):
            rows = w1[KP * g : KP * (g + 1), :].rearrange("(p i) c -> p i c", i=PACK)
            load(w1_in[g][:, 2 * u : 2 * u + 2, :], rows[:, 2 * u : 2 * u + 2, :])

        def load_words(dst, words):
            load_raw(dst[:], words.rearrange("p t i -> p (t i)"))

        load(lists[0][:], offs)
        load_raw(w4_in[:], w4_words.rearrange("a p n -> p a n"))
        load(lists[1][:], offs2)
        load(lists[2][:], offs3)
        load(gains[:], gain.rearrange("(a p t) -> p a t", a=2, t=PACK))
        load_w1(0, 0)
        load_small(0, 6)
        load_w1(0, 1)
        load_w1(1, 0)
        load_small(6, 12)
        load_words(tab_w[2], tab_words[2])
        load_w1(1, 1)
        load_small(12, 16)
        load_words(tab_w[3], tab_words[3])
        load_words(tab_w[0], tab_words[0])
        load_words(tab_w[1], tab_words[1])
        for a in range(2):
            rows = level[KP * a : KP * (a + 1), :].rearrange("(p t) j -> p t j", t=PACK)
            for u in range(2):
                load(lev[a][u][:], rows[:, 2 * u : 2 * u + 2, :])
        for n, words in enumerate((tab2_words, tab3_words)):
            for a in range(2):
                load_words(crew_w[n][a], words[a])
        for u in range(2):
            load(seats[u][:], seat[2 * P * u : 2 * P * (u + 1), :].rearrange("(q p) j -> p q j", q=2))

        w4_codes = tile("w4_codes", [P, 2, 2 * H], U8)
        nc.vector.tensor_copy(
            out=w4_codes[:].bitcast(U16).rearrange("p g (a t m) -> p (g a) t m", a=2, t=PACK),
            in_=w4_in[:].bitcast(U16).rearrange("p g (a m t) -> p (g a) t m", a=2, t=PACK),
        )

        def gather(name, window, n, dtype, over):
            picked = tile(name, [P, S], dtype, over)
            nc.vector.tensor_copy(out=picked[:], in_=window.indirect(lists[n][:]))
            return picked

        w1_codes = [[None, None], [None, None]]
        w1_sc = [[None, None], [None, None]]

        def quantise_w1(g, a, over=None):
            grouped = tile("w1_bf%d%d" % (g, a), [P, KP * PACK], BF16)
            nc.scalar.copy(
                out=grouped[:].rearrange("p (t m i) -> p m t i", t=PACK, i=PACK),
                in_=w1_in[g][:, :, KP * a : KP * (a + 1)].rearrange("p i (m t) -> p m t i", t=PACK),
            )
            w1_codes[g][a] = tile("w1_codes%d%d" % (g, a), [P, KP], U32, over)
            w1_sc[g][a] = tile("w1_sc%d%d" % (g, a), [P, KP], U8)
            nc.vector.quantize_mx(out=w1_codes[g][a][:].bitcast(FP8X4), scales=w1_sc[g][a][:], in_=grouped[:])

        v = [None] * 4
        w4_sc = tile("w4_sc", [P, 2, H], U8)
        nc.vector.tensor_copy(
            out=w4_sc[:].rearrange("p g (a t m) -> p (g a) t m", a=2, t=PACK),
            in_=w4_sc_in[:].rearrange("p g (a m t) -> p (g a) t m", a=2, t=PACK),
        )
        quantise_w1(0, 0)
        crew_scales = [None, gather("crew_scales1", crew_sc[1][:], 2, U8, "w4_sc_in")]
        v_sc = [gather("v_sc0", tab_sc[:, 0, :], 0, U8, "crew_sc1"), gather("v_sc1", tab_sc[:, 1, :], 0, U8, "w4_in")]
        v[2] = gather("v2", tab_w[2][:], 0, U32, "tab_sc")
        quantise_w1(0, 1, "tab_w2")
        crew_scales[0] = gather("crew_scales0", crew_sc[0][:], 1, U8, "w1_bf01")
        v[3] = gather("v3", tab_w[3][:], 0, U32, "crew_sc0")
        quantise_w1(1, 0, "tab_w3")
        v[0] = gather("v0", tab_w[0][:], 0, U32, "w1_bf10")
        quantise_w1(1, 1, "tab_w0")
        v[1] = gather("v1", tab_w[1][:], 0, U32, "w1_bf11")

        f = [[psum.tile([P, S], F32, name="bank%d" % (PACK * a + t)) for t in range(PACK)] for a in range(2)]
        for g in (2, 3, 0, 1):
            for a in range(2):
                for t in range(PACK):
                    if g < 2:
                        cols = slice(P * t, P * (t + 1))
                        codes = w1_codes[g][a][:, cols].bitcast(FP8X4)
                        scales = w1_sc[g][a][:, cols]
                        rhs_scale = v_sc[g][4:P, :]
                    else:
                        c0 = KP * a + P * t
                        codes = w4_codes[:, g - 2, 2 * c0 : 2 * (c0 + P)].bitcast(FP4X4)
                        scales = w4_sc[:, g - 2, c0 : c0 + P]
                        rhs_scale = v_sc[g - 2][:]
                    nc.tensor.matmul_mx(
                        out=f[a][t][:], lhsT=codes, lhsT_scale=scales,
                        rhs=v[g][:].bitcast(FP8X4), rhs_scale=rhs_scale, start=(g == 2), stop=(g == 1),
                    )

        lifted = [[tile("lifted%d%d" % (a, t), [P, S], F32) for t in range(PACK)] for a in range(2)]
        for a in range(2):
            for t in range(PACK):
                nc.vector.tensor_tensor(out=lifted[a][t][:], in0=f[a][t][:], in1=lev[a][t // 2][:, t % 2, :], op=ALU.max)

        def make_h(a, j0, width, name):
            scaled = tile("scaled" + name, [P, PACK, width], BF16)
            for t in range(PACK):
                nc.scalar.activation(
                    out=scaled[:, t, :], in_=lifted[a][t][:, j0 : j0 + width], func=COPY, scale=gains[:, a, t : t + 1]
                )
            grouped = tile("h_bf" + name, [P, PACK * width], BF16)
            nc.scalar.copy(
                out=grouped[:].rearrange("p (j t) -> p j t", t=PACK),
                in_=scaled[:].rearrange("p t j -> p j t"),
            )
            return grouped

        def quantise_h(grouped, width, name, over):
            codes = tile("h_codes" + name, [P, width], U32, over)
            scales = tile("h_sc" + name, [P, width], U8)
            nc.vector.quantize_mx(out=codes[:].bitcast(FP8X4), scales=scales[:], in_=grouped[:])
            return codes, scales

        h_first = make_h(0, 0, S, "a")
        h_second = [make_h(1, HALF * jh, HALF, "b%d" % jh) for jh in range(2)]
        crew = [[None, None], [None, None]]
        e = [
            [[psum.tile([P, 2, HALF], F32, name="bank%d" % (4 * jh + 2 * n + u)) for u in range(2)] for n in range(2)]
            for jh in range(2)
        ]

        def score(jh, n, a, codes, scales):
            for u in range(2):
                for q in range(2):
                    cols = slice(P * (2 * u + q), P * (2 * u + q + 1))
                    nc.tensor.matmul_mx(
                        out=e[jh][n][u][:, q, :], lhsT=crew[n][a][:, cols].bitcast(FP8X4),
                        lhsT_scale=crew_scales[n][8 + 4 * a : P, cols],
                        rhs=codes.bitcast(FP8X4), rhs_scale=scales,
                        start=(a, q) == (0, 0), stop=(a, q) == (1, 1),
                    )

        halves = [slice(HALF * jh, HALF * (jh + 1)) for jh in range(2)]
        crew[0][0] = gather("crew00", crew_w[0][0][:], 1, U32, "lev10")
        crew[0][1] = gather("crew01", crew_w[0][1][:], 1, U32, "lev11")
        codes_a, scales_a = quantise_h(h_first, S, "a", None)
        for jh in range(2):
            score(jh, 0, 0, codes_a[:, halves[jh]], scales_a[:, halves[jh]])
        crew[1][0] = gather("crew10", crew_w[1][0][:], 2, U32, "h_bfa")
        for jh in range(2):
            score(jh, 1, 0, codes_a[:, halves[jh]], scales_a[:, halves[jh]])
        codes_b, scales_b = quantise_h(h_second[0], HALF, "b0", None)
        score(0, 0, 1, codes_b[:], scales_b[:])
        crew[1][1] = gather("crew11", crew_w[1][1][:], 2, U32, "h_bfb0")
        score(0, 1, 1, codes_b[:], scales_b[:])

        for jh in range(2):
            jcols = halves[jh]
            first = [ring.tile([P, 2, HALF], F32, name="first%d" % u) for u in range(2)]
            for u in range(2):
                nc.vector.scalar_tensor_tensor(
                    out=first[u][:], in0=seats[u][:, :, jcols], scalar=2.0, in1=e[jh][0][u][:], op0=ALU.mult, op1=ALU.add
                )
            if jh == 0:
                codes_b, scales_b = quantise_h(h_second[1], HALF, "b1", None)
                for n in range(2):
                    score(1, n, 1, codes_b[:], scales_b[:])
            for u in range(2):
                best = tile("best%d%d" % (jh, u), [P, 2, HALF], F32, "h_bfb1" if (jh, u) == (0, 1) else None)
                nc.vector.tensor_tensor(out=best[:], in0=e[jh][1][u][:], in1=first[u][:], op=ALU.max)
                result = ring.tile([P, 2, HALF], F32, name="result%d" % u)
                engine = nc.vector if (jh, u) == (1, 1) else nc.gpsimd
                engine.tensor_tensor(out=result[:], in0=best[:], in1=seats[u][:, :, jcols], op=ALU.subtract)
                nc.sync.dma_start(
                    out=out[2 * P * u : 2 * P * (u + 1), jcols].rearrange("(q p) j -> p q j", q=2), in_=result[:]
                )
